import numpy as np
import ml_dtypes


def mxq(x, axis, fmt="e4m3"):
    dtype, down = {"e4m3": (ml_dtypes.float8_e4m3fn, 7), "e5m2": (ml_dtypes.float8_e5m2, 14)}[fmt]
    v = np.moveaxis(np.asarray(x, np.float32).astype(ml_dtypes.bfloat16).astype(np.float64), axis, -1)
    blocks = v.reshape(v.shape[:-1] + (-1, 32))
    amax = np.abs(blocks).max(-1, keepdims=True)
    byte = np.maximum(np.where(amax > 0, np.frexp(amax)[1] - 1 + 127, 0) - down, 1)
    scale = np.exp2(byte - 127.0)
    codes = (blocks / scale).astype(np.float32).astype(dtype).astype(np.float64)
    return np.moveaxis((codes * scale).reshape(v.shape), -1, axis)


WIDE = False


def mx_kscale(k):
    if not WIDE:
        return np.ones(k)
    levels = np.array([10, -10, 5, -5, 0])
    if k % 512:
        return np.exp2(np.random.permutation(np.resize(levels, k // 32))).repeat(32)
    a = np.empty((k // 512, 16))
    for p in range(k // 512):
        a[p, :8] = np.random.permutation(np.resize(levels, 8))
        for g in range(8):
            far = levels[np.abs(levels - a[p, g]) >= 10]
            a[p, g + 8] = far[np.random.randint(len(far))]
    return np.exp2(a.ravel()).repeat(32)


def f64(x):
    return np.asarray(x).astype(np.float64)


def striped(idx):
    return np.tile(idx.reshape(-1, 16).T, (8, 1)).astype(np.uint16)


def unstriped(offs):
    return offs[:16].T.reshape(-1).astype(np.int64)


def pack_weight(w):
    k, n = w.shape
    w = f64(np.asarray(w, np.float32).astype(ml_dtypes.bfloat16)).reshape(k // 32, 32, n)
    amax = np.abs(w).max(1)
    byte = np.clip(np.where(amax > 0, np.frexp(amax)[1] - 1 + 127 - 7, 1), 1, 254)
    scaled = (w * np.exp2(127.0 - byte)[:, None, :]).reshape(k, n).astype(np.float32)
    words = np.ascontiguousarray(scaled.reshape(k // 512, 128, 4, n).transpose(0, 1, 3, 2)).astype(ml_dtypes.float8_e4m3fn).view(np.uint8)
    return words, np.ascontiguousarray(byte.astype(np.uint8).reshape(k // 512, 16, n))


def unpack_weight(words, scales):
    g, p, n, _ = words.shape
    vals = np.ascontiguousarray(words).view(ml_dtypes.float8_e4m3fn).astype(np.float64) * np.repeat(np.exp2(scales.astype(np.float64) - 127.0), 8, axis=1)[..., None]
    return vals.transpose(0, 1, 3, 2).reshape(g * 512, n)


def relu(v):
    return np.maximum(v, 0.0)

def planes(y):
    n, m = y.shape
    v = y.astype(np.float32).astype(ml_dtypes.bfloat16).astype(np.float64).reshape(n // 32, 32, m)
    top = np.abs(v).max(1)
    byte = np.clip(np.where(top > 0, np.frexp(top)[1] - 1 + 127 - 7, 1), 1, 254)
    codes = (v * np.exp2(127.0 - byte)[:, None, :]).reshape(n, m).astype(np.float32).astype(ml_dtypes.float8_e4m3fn).view(np.uint8)
    words = codes.reshape(n // 512, 128, 4, m).transpose(0, 1, 3, 2)
    return np.ascontiguousarray(words), np.ascontiguousarray(byte.astype(np.uint8).reshape(n // 512, 16, m))


K, T, S, N, H = 512, 2048, 512, 512, 512


def setup_inputs():
    n = np.random.standard_normal
    s = mx_kscale(K)[:, None]
    u = mx_kscale(S)
    packed_xT = pack_weight(n((K, T)) * s)
    packed_w1 = pack_weight(n((S, N)) / np.sqrt(S) / u[:, None])
    return {
        "x_words": packed_xT[0],
        "x_scales": packed_xT[1],
        "wa": (n((K, H)) / np.sqrt(K) / s).astype(np.float32),
        "wb": (n((K, H)) / np.sqrt(K) / s).astype(np.float32),
        "gt": (np.random.uniform(0.5, 1.5, (S, 1)) * u[:, None]).astype(np.float32),
        "reg": n((N, H)).astype(np.float32),
        "w1_words": packed_w1[0],
        "w1_scales": packed_w1[1],
        "offs": striped(np.random.permutation(T)[:S]),
    }


def reference(x_words, x_scales, wa, wb, gt, reg, w1_words, w1_scales, offs):
    xq = unpack_weight(x_words, x_scales)[:, unstriped(offs)]
    a = xq.T @ mxq(f64(wa), 0, "e4m3")
    b = xq.T @ mxq(f64(wb), 0, "e4m3")
    z = f64(gt) * (relu(a) * b)
    out_0 = f64(reg) + (unpack_weight(w1_words, w1_scales).T @ mxq(z, 0, "e4m3"))
    return (out_0,) + planes(out_0)

@@ -1,0 +1,203 @@
+from contextlib import ExitStack
+
+import concourse.mybir as mybir
+
+K, T, S, N, H = 512, 2048, 512, 512, 512
+FLOPS = 2 * S * K * H * 2 + 2 * S * N * H
+
+F32 = mybir.dt.float32
+BF16 = mybir.dt.bfloat16
+I32 = mybir.dt.int32
+U32 = mybir.dt.uint32
+U16 = mybir.dt.uint16
+U8 = mybir.dt.uint8
+FP8X4 = mybir.dt.float8_e4m3fn_x4
+COPY = mybir.ActivationFunctionType.Copy
+ALU = mybir.AluOpType
+
+P = 128
+PACK = 4
+CHUNK = 128
+CHUNKS = H // CHUNK
+LINE = 4
+
+
+def round_and_interleave(nc, on_scalar, out, in_):
+    dst = out.rearrange("p (c i) t -> p c t i", i=LINE)
+    src = in_.rearrange("p t (c i) -> p c t i", i=LINE)
+    if on_scalar:
+        nc.scalar.activation(out=dst, in_=src, func=COPY)
+    else:
+        nc.vector.tensor_copy(out=dst, in_=src)
+
+
+def quantize(nc, codes, scales, values):
+    nc.vector.quantize_mx(out=codes.bitcast(FP8X4), scales=scales, in_=values)
+
+
+def four_products(nc, bank, lhs_codes, lhs_scales, rhs_codes, rhs_scales):
+    for t in range(PACK):
+        cols = slice(t * P, (t + 1) * P)
+        nc.tensor.matmul_mx(
+            out=bank[:, t, :],
+            lhsT=lhs_codes[:, cols].bitcast(FP8X4),
+            lhsT_scale=lhs_scales[:, cols],
+            rhs=rhs_codes.bitcast(FP8X4),
+            rhs_scale=rhs_scales,
+            start=True,
+            stop=True,
+        )
+
+
+def tile_picked_regmix_relu_po_kernel(
+    tc, x_words, x_scales, wa, wb, gt, reg, w1_words, w1_scales, offs, out_0, out_1, out_2
+):
+    nc = tc.nc
+    with ExitStack() as ctx:
+        keep = ctx.enter_context(tc.tile_pool(name="keep", bufs=1))
+        ring = ctx.enter_context(tc.tile_pool(name="ring", bufs=CHUNKS))
+        psum_ab = ctx.enter_context(tc.psum_pool(name="psum_ab", bufs=3))
+        psum_o = ctx.enter_context(tc.psum_pool(name="psum_o", bufs=2))
+
+        wa_rows = wa.rearrange("(p t) j -> p t j", t=PACK)
+        wb_rows = wb.rearrange("(p t) j -> p t j", t=PACK)
+        reg_rows = reg.rearrange("(p t) j -> p t j", t=PACK)
+        out_rows = out_0.rearrange("(p t) j -> p t j", t=PACK)
+        out_words = out_1[0].rearrange("p j t -> p (j t)").bitcast(I32)
+
+        offsets = keep.tile([P, S // 16], U16, name="offsets")
+        x_word_table = keep.tile([P, T], I32, name="x_word_table", align_bytes=64)
+        x_scale_table = keep.tile([P, T], U8, name="x_scale_table", align_bytes=64)
+        w1_raw_words = keep.tile([P, N], I32, name="w1_raw_words", align_bytes=64)
+        w1_raw_scales = keep.tile([P, N], U8, name="w1_raw_scales", align_bytes=64)
+        gate = keep.tile([P, PACK], F32, name="gate")
+
+        wa_raw, wb_raw, reg_raw = [], [], []
+
+        def load_weights(c):
+            cols = slice(c * CHUNK, (c + 1) * CHUNK)
+            wa_c = ring.tile([P, PACK, CHUNK], F32, name="wa_c", align_bytes=64)
+            wb_c = ring.tile([P, PACK, CHUNK], F32, name="wb_c", align_bytes=64)
+            nc.sync.dma_start(out=wb_c[:], in_=wb_rows[:, :, cols])
+            nc.sync.dma_start(out=wa_c[:], in_=wa_rows[:, :, cols])
+            wa_raw.append(wa_c)
+            wb_raw.append(wb_c)
+
+        def load_reg(c):
+            cols = slice(c * CHUNK, (c + 1) * CHUNK)
+            reg_c = ring.tile([P, PACK, CHUNK], F32, name="reg_c", align_bytes=64)
+            nc.sync.dma_start(out=reg_c[:], in_=reg_rows[:, :, cols])
+            reg_raw.append(reg_c)
+
+        nc.vector.memset(x_scale_table[:].bitcast(I32), 0)
+        nc.gpsimd.memset(w1_raw_scales[:].bitcast(I32), 0)
+        nc.sync.dma_start(offsets[:], offs)
+        for q in range(4):
+            nc.scalar.dma_start(
+                out=x_scale_table[32 * q : 32 * q + 4, :].bitcast(I32),
+                in_=x_scales[0, 4 * q : 4 * q + 4, :].bitcast(I32),
+            )
+        load_weights(0)
+        nc.sync.dma_start(out=x_word_table[:], in_=x_words[0].rearrange("p c t -> p (c t)").bitcast(I32))
+        nc.sync.dma_start(out=gate[:], in_=gt.rearrange("(p t) o -> p (t o)", t=PACK))
+        load_weights(1)
+        for q in range(4):
+            nc.sync.dma_start(
+                out=w1_raw_scales[32 * q : 32 * q + 4, :].bitcast(I32),
+                in_=w1_scales[0, 4 * q : 4 * q + 4, :].bitcast(I32),
+            )
+        nc.sync.dma_start(out=w1_raw_words[:], in_=w1_words[0].rearrange("p c t -> p (c t)").bitcast(I32))
+        for c in range(2, CHUNKS):
+            load_weights(c)
+            load_reg(c - 2)
+        load_reg(CHUNKS - 2)
+        load_reg(CHUNKS - 1)
+
+        picked_scales = keep.tile([P, S], U8, name="picked_scales", align_bytes=64)
+        x_codes = keep.tile([P, S], U32, name="x_codes", align_bytes=64)
+        x_plane = keep.tile([P, S], U8, name="x_plane", align_bytes=64)
+        w1_codes = keep.tile([P, N], I32, name="w1_codes", align_bytes=64)
+        w1_plane = keep.tile([P, N], U8, name="w1_plane", align_bytes=64)
+        out_plane = keep.tile([P, H], U8, name="out_plane", align_bytes=64)
+
+        nc.vector.tensor_copy(out=picked_scales[:], in_=x_scale_table[:].indirect(offsets[:]))
+        nc.vector.tensor_copy(
+            out=x_plane[:].rearrange("p (t m) -> p t m", t=PACK),
+            in_=picked_scales[:].rearrange("p (m t) -> p t m", t=PACK),
+        )
+
+        banks, products = {}, {}
+
+        def first_products(c):
+            w_bf16 = ring.tile([P, 2, CHUNK, PACK], BF16, name="w_bf16", align_bytes=64)
+            w_codes = ring.tile([P, 2 * CHUNK], U32, name="w_codes", align_bytes=64)
+            w_plane = ring.tile([P, 2 * CHUNK], U8, name="w_plane", align_bytes=64)
+            round_and_interleave(nc, True, w_bf16[:, 0, :, :], wb_raw[c][:])
+            round_and_interleave(nc, True, w_bf16[:, 1, :, :], wa_raw[c][:])
+            quantize(nc, w_codes[:], w_plane[:], w_bf16[:].rearrange("p m j t -> p (m j t)"))
+            if c == 0:
+                nc.vector.tensor_copy(
+                    out=x_codes[:].rearrange("p (t m) -> p m t", t=PACK),
+                    in_=x_word_table[:].bitcast(U32).indirect(offsets[:]),
+                )
+            b_bank = psum_ab.tile([P, PACK, CHUNK], F32, name="b_bank")
+            a_bank = psum_ab.tile([P, PACK, CHUNK], F32, name="a_bank")
+            four_products(nc, b_bank, x_codes, x_plane, w_codes[:, :CHUNK], w_plane[:, :CHUNK])
+            four_products(nc, a_bank, x_codes, x_plane, w_codes[:, CHUNK:], w_plane[:, CHUNK:])
+            banks[c] = (a_bank, b_bank)
+
+        def gated_product(c):
+            a_bank, b_bank = banks[c]
+            gated_b = ring.tile([P, PACK, CHUNK], F32, name="gated_b", align_bytes=64)
+            for t in range(PACK):
+                nc.scalar.activation(out=gated_b[:, t, :], in_=b_bank[:, t, :], func=COPY, scale=gate[:, t : t + 1])
+            z_bf16 = ring.tile([P, CHUNK, PACK], BF16, name="z_bf16", align_bytes=64)
+            nc.vector.scalar_tensor_tensor(
+                out=z_bf16[:],
+                in0=a_bank[:].rearrange("p t j -> p j t"),
+                scalar=0.0,
+                in1=gated_b[:].rearrange("p t j -> p j t"),
+                op0=ALU.max,
+                op1=ALU.mult,
+            )
+            if c == 0:
+                nc.vector.tensor_copy(
+                    out=w1_codes[:].rearrange("p (t m) -> p t m", t=PACK),
+                    in_=w1_raw_words[:].rearrange("p (m t) -> p t m", t=PACK),
+                )
+                nc.vector.tensor_copy(
+                    out=w1_plane[:].rearrange("p (t m) -> p t m", t=PACK),
+                    in_=w1_raw_scales[:].rearrange("p (m t) -> p t m", t=PACK),
+                )
+            z_codes = ring.tile([P, CHUNK], U32, name="z_codes", align_bytes=64)
+            z_plane = ring.tile([P, CHUNK], U8, name="z_plane", align_bytes=64)
+            quantize(nc, z_codes[:], z_plane[:], z_bf16[:].rearrange("p j t -> p (j t)"))
+            o_bank = psum_o.tile([P, PACK, CHUNK], F32, name="o_bank")
+            four_products(nc, o_bank, w1_codes, w1_plane, z_codes[:], z_plane[:])
+            products[c] = o_bank
+
+        def hand_out(c):
+            cols = slice(c * CHUNK, (c + 1) * CHUNK)
+            y = ring.tile([P, PACK, CHUNK], F32, name="y", align_bytes=64)
+            nc.vector.tensor_tensor(out=y[:], in0=products[c][:], in1=reg_raw[c][:], op=ALU.add)
+            nc.sync.dma_start(out=out_rows[:, :, cols], in_=y[:])
+            y_bf16 = ring.tile([P, CHUNK, PACK], BF16, name="y_bf16", align_bytes=64)
+            round_and_interleave(nc, c > 0, y_bf16[:], y[:])
+            y_codes = ring.tile([P, CHUNK], I32, name="y_codes", align_bytes=64)
+            quantize(nc, y_codes[:], out_plane[:, cols], y_bf16[:].rearrange("p j t -> p (j t)"))
+            nc.sync.dma_start(out=out_words[:, cols], in_=y_codes[:])
+
+        for step in range(CHUNKS + 2):
+            if 0 <= step - 2 < CHUNKS:
+                hand_out(step - 2)
+            if 0 <= step - 1 < CHUNKS:
+                gated_product(step - 1)
+            if step < CHUNKS:
+                first_products(step)
+
+        for q in range(4):
+            queue = nc.sync if q % 2 == 0 else nc.scalar
+            queue.dma_start(
+                out=out_2[0, 4 * q : 4 * q + 4, :].bitcast(I32),
+                in_=out_plane[32 * q : 32 * q + 4, :].bitcast(I32),
+            )

@@ -17,9 +17,11 @@ ALU = mybir.AluOpType
 
 P = 128
 PACK = 4
-CHUNK = 128
-CHUNKS = H // CHUNK
 LINE = 4
+WIDTHS = [128,128,128,128]
+STARTS = [sum(WIDTHS[:c]) for c in range(len(WIDTHS))]
+CHUNKS = len(WIDTHS)
+Y_ON_VECTOR = [0,3]
 
 
 def round_and_interleave(nc, on_scalar, out, in_):
@@ -32,7 +34,7 @@ def round_and_interleave(nc, on_scalar, out, in_):
 
 
 def quantize(nc, codes, scales, values):
-    nc.vector.quantize_mx(out=codes.bitcast(FP8X4), scales=scales, in_=values)
+    nc.vector.quantize_mx(out=codes.bitcast(FP8X4), scales=scales, in_=values.rearrange("p j t -> p (j t)"))
 
 
 def four_products(nc, bank, lhs_codes, lhs_scales, rhs_codes, rhs_scales):
@@ -72,46 +74,45 @@ def tile_picked_regmix_relu_po_kernel(
         w1_raw_scales = keep.tile([P, N], U8, name="w1_raw_scales", align_bytes=64)
         gate = keep.tile([P, PACK], F32, name="gate")
 
-        wa_raw, wb_raw, reg_raw = [], [], []
+        wa_raw, wb_raw, reg_raw = {}, {}, {}
 
-        def load_weights(c):
-            cols = slice(c * CHUNK, (c + 1) * CHUNK)
-            wa_c = ring.tile([P, PACK, CHUNK], F32, name="wa_c", align_bytes=64)
-            wb_c = ring.tile([P, PACK, CHUNK], F32, name="wb_c", align_bytes=64)
-            nc.sync.dma_start(out=wb_c[:], in_=wb_rows[:, :, cols])
-            nc.sync.dma_start(out=wa_c[:], in_=wa_rows[:, :, cols])
-            wa_raw.append(wa_c)
-            wb_raw.append(wb_c)
+        def load_chunks(rows, loaded, name, first, count):
+            lo = STARTS[first]
+            hi = STARTS[first + count - 1] + WIDTHS[first + count - 1]
+            raw = keep.tile([P, PACK, hi - lo], F32, name="%s%d" % (name, first), align_bytes=64)
+            nc.sync.dma_start(out=raw[:], in_=rows[:, :, lo:hi])
+            for c in range(first, first + count):
+                loaded[c] = raw[:, :, STARTS[c] - lo : STARTS[c] - lo + WIDTHS[c]]
 
-        def load_reg(c):
-            cols = slice(c * CHUNK, (c + 1) * CHUNK)
-            reg_c = ring.tile([P, PACK, CHUNK], F32, name="reg_c", align_bytes=64)
-            nc.sync.dma_start(out=reg_c[:], in_=reg_rows[:, :, cols])
-            reg_raw.append(reg_c)
+        def load_scales(plane, scales):
+            for q in range(4):
+                nc.sync.dma_start(
+                    out=plane[32 * q : 32 * q + 4, :].bitcast(I32),
+                    in_=scales[0, 4 * q : 4 * q + 4, :].bitcast(I32),
+                )
 
-        nc.vector.memset(x_scale_table[:].bitcast(I32), 0)
+        def load_words(table, words):
+            nc.sync.dma_start(out=table[:], in_=words[0].rearrange("p c t -> p (c t)").bitcast(I32))
+
+        nc.vector.memset(x_scale_table[:, : T // 2].bitcast(I32), 0)
+        nc.gpsimd.memset(x_scale_table[:, T // 2 :].bitcast(I32), 0)
         nc.gpsimd.memset(w1_raw_scales[:].bitcast(I32), 0)
         nc.sync.dma_start(offsets[:], offs)
-        for q in range(4):
-            nc.scalar.dma_start(
-                out=x_scale_table[32 * q : 32 * q + 4, :].bitcast(I32),
-                in_=x_scales[0, 4 * q : 4 * q + 4, :].bitcast(I32),
-            )
-        load_weights(0)
-        nc.sync.dma_start(out=x_word_table[:], in_=x_words[0].rearrange("p c t -> p (c t)").bitcast(I32))
         nc.sync.dma_start(out=gate[:], in_=gt.rearrange("(p t) o -> p (t o)", t=PACK))
-        load_weights(1)
-        for q in range(4):
-            nc.sync.dma_start(
-                out=w1_raw_scales[32 * q : 32 * q + 4, :].bitcast(I32),
-                in_=w1_scales[0, 4 * q : 4 * q + 4, :].bitcast(I32),
-            )
-        nc.sync.dma_start(out=w1_raw_words[:], in_=w1_words[0].rearrange("p c t -> p (c t)").bitcast(I32))
-        for c in range(2, CHUNKS):
-            load_weights(c)
-            load_reg(c - 2)
-        load_reg(CHUNKS - 2)
-        load_reg(CHUNKS - 1)
+        load_scales(x_scale_table, x_scales)
+        load_chunks(wb_rows, wb_raw, "wb_raw", 0, 1)
+        load_words(x_word_table, x_words)
+        load_chunks(wa_rows, wa_raw, "wa_raw", 0, 1)
+        load_chunks(wb_rows, wb_raw, "wb_raw", 1, 1)
+        load_chunks(wa_rows, wa_raw, "wa_raw", 1, 1)
+        load_scales(w1_raw_scales, w1_scales)
+        load_words(w1_raw_words, w1_words)
+        load_chunks(wb_rows, wb_raw, "wb_raw", 2, 1)
+        load_chunks(wa_rows, wa_raw, "wa_raw", 2, 1)
+        load_chunks(wb_rows, wb_raw, "wb_raw", 3, 1)
+        load_chunks(wa_rows, wa_raw, "wa_raw", 3, 1)
+        load_chunks(reg_rows, reg_raw, "reg_raw", 0, 2)
+        load_chunks(reg_rows, reg_raw, "reg_raw", 2, 2)
 
         picked_scales = keep.tile([P, S], U8, name="picked_scales", align_bytes=64)
         x_codes = keep.tile([P, S], U32, name="x_codes", align_bytes=64)
@@ -120,80 +121,99 @@ def tile_picked_regmix_relu_po_kernel(
         w1_plane = keep.tile([P, N], U8, name="w1_plane", align_bytes=64)
         out_plane = keep.tile([P, H], U8, name="out_plane", align_bytes=64)
 
+        def deal(out, in_):
+            nc.vector.tensor_copy(
+                out=out[:].rearrange("p (t m) -> p t m", t=PACK),
+                in_=in_[:].rearrange("p (m t) -> p t m", t=PACK),
+            )
+
         nc.vector.tensor_copy(out=picked_scales[:], in_=x_scale_table[:].indirect(offsets[:]))
+        deal(x_plane, picked_scales)
         nc.vector.tensor_copy(
-            out=x_plane[:].rearrange("p (t m) -> p t m", t=PACK),
-            in_=picked_scales[:].rearrange("p (m t) -> p t m", t=PACK),
+            out=x_codes[:].rearrange("p (t m) -> p m t", t=PACK),
+            in_=x_word_table[:].bitcast(U32).indirect(offsets[:]),
         )
 
-        banks, products = {}, {}
+        a_banks, b_banks, z_values, products, y_values = {}, {}, {}, {}, {}
 
-        def first_products(c):
-            w_bf16 = ring.tile([P, 2, CHUNK, PACK], BF16, name="w_bf16", align_bytes=64)
-            w_codes = ring.tile([P, 2 * CHUNK], U32, name="w_codes", align_bytes=64)
-            w_plane = ring.tile([P, 2 * CHUNK], U8, name="w_plane", align_bytes=64)
-            round_and_interleave(nc, True, w_bf16[:, 0, :, :], wb_raw[c][:])
-            round_and_interleave(nc, True, w_bf16[:, 1, :, :], wa_raw[c][:])
-            quantize(nc, w_codes[:], w_plane[:], w_bf16[:].rearrange("p m j t -> p (m j t)"))
-            if c == 0:
-                nc.vector.tensor_copy(
-                    out=x_codes[:].rearrange("p (t m) -> p m t", t=PACK),
-                    in_=x_word_table[:].bitcast(U32).indirect(offsets[:]),
-                )
-            b_bank = psum_ab.tile([P, PACK, CHUNK], F32, name="b_bank")
-            a_bank = psum_ab.tile([P, PACK, CHUNK], F32, name="a_bank")
-            four_products(nc, b_bank, x_codes, x_plane, w_codes[:, :CHUNK], w_plane[:, :CHUNK])
-            four_products(nc, a_bank, x_codes, x_plane, w_codes[:, CHUNK:], w_plane[:, CHUNK:])
-            banks[c] = (a_bank, b_bank)
+        def weight_products(raw, name, c):
+            width = WIDTHS[c]
+            w_bf16 = ring.tile([P, width, PACK], BF16, name=name + "_bf16", align_bytes=64)
+            w_codes = ring.tile([P, width], U32, name=name + "_codes", align_bytes=64)
+            w_plane = ring.tile([P, width], U8, name=name + "_plane", align_bytes=64)
+            round_and_interleave(nc, True, w_bf16[:], raw)
+            quantize(nc, w_codes[:], w_plane[:], w_bf16[:])
+            bank = psum_ab.tile([P, PACK, width], F32, name=name + "_bank")
+            four_products(nc, bank, x_codes, x_plane, w_codes[:], w_plane[:])
+            return bank
 
-        def gated_product(c):
-            a_bank, b_bank = banks[c]
-            gated_b = ring.tile([P, PACK, CHUNK], F32, name="gated_b", align_bytes=64)
+        def b_products(c):
+            b_banks[c] = weight_products(wb_raw[c], "b", c)
+
+        def a_products(c):
+            a_banks[c] = weight_products(wa_raw[c], "a", c)
+
+        def gated(c):
+            width = WIDTHS[c]
+            gated_b = wb_raw[(c + 1) % CHUNKS]
             for t in range(PACK):
-                nc.scalar.activation(out=gated_b[:, t, :], in_=b_bank[:, t, :], func=COPY, scale=gate[:, t : t + 1])
-            z_bf16 = ring.tile([P, CHUNK, PACK], BF16, name="z_bf16", align_bytes=64)
+                nc.scalar.activation(out=gated_b[:, t, :], in_=b_banks[c][:, t, :], func=COPY, scale=gate[:, t : t + 1])
+            z_bf16 = ring.tile([P, width, PACK], BF16, name="z_bf16", align_bytes=64)
             nc.vector.scalar_tensor_tensor(
                 out=z_bf16[:],
-                in0=a_bank[:].rearrange("p t j -> p j t"),
+                in0=a_banks[c][:].rearrange("p t j -> p j t"),
                 scalar=0.0,
-                in1=gated_b[:].rearrange("p t j -> p j t"),
+                in1=gated_b.rearrange("p t j -> p j t"),
                 op0=ALU.max,
                 op1=ALU.mult,
             )
-            if c == 0:
-                nc.vector.tensor_copy(
-                    out=w1_codes[:].rearrange("p (t m) -> p t m", t=PACK),
-                    in_=w1_raw_words[:].rearrange("p (m t) -> p t m", t=PACK),
-                )
-                nc.vector.tensor_copy(
-                    out=w1_plane[:].rearrange("p (t m) -> p t m", t=PACK),
-                    in_=w1_raw_scales[:].rearrange("p (m t) -> p t m", t=PACK),
-                )
-            z_codes = ring.tile([P, CHUNK], U32, name="z_codes", align_bytes=64)
-            z_plane = ring.tile([P, CHUNK], U8, name="z_plane", align_bytes=64)
-            quantize(nc, z_codes[:], z_plane[:], z_bf16[:].rearrange("p j t -> p (j t)"))
-            o_bank = psum_o.tile([P, PACK, CHUNK], F32, name="o_bank")
+            z_values[c] = z_bf16
+
+        def second_product(c):
+            width = WIDTHS[c]
+            z_codes = ring.tile([P, width], U32, name="z_codes", align_bytes=64)
+            z_plane = ring.tile([P, width], U8, name="z_plane", align_bytes=64)
+            quantize(nc, z_codes[:], z_plane[:], z_values[c][:])
+            o_bank = psum_o.tile([P, PACK, width], F32, name="o_bank")
             four_products(nc, o_bank, w1_codes, w1_plane, z_codes[:], z_plane[:])
             products[c] = o_bank
 
-        def hand_out(c):
-            cols = slice(c * CHUNK, (c + 1) * CHUNK)
-            y = ring.tile([P, PACK, CHUNK], F32, name="y", align_bytes=64)
-            nc.vector.tensor_tensor(out=y[:], in0=products[c][:], in1=reg_raw[c][:], op=ALU.add)
+        def add_reg(c):
+            width = WIDTHS[c]
+            cols = slice(STARTS[c], STARTS[c] + width)
+            y = ring.tile([P, PACK, width], F32, name="y", align_bytes=64)
+            nc.vector.tensor_tensor(out=y[:], in0=products[c][:], in1=reg_raw[c], op=ALU.add)
             nc.sync.dma_start(out=out_rows[:, :, cols], in_=y[:])
-            y_bf16 = ring.tile([P, CHUNK, PACK], BF16, name="y_bf16", align_bytes=64)
-            round_and_interleave(nc, c > 0, y_bf16[:], y[:])
-            y_codes = ring.tile([P, CHUNK], I32, name="y_codes", align_bytes=64)
-            quantize(nc, y_codes[:], out_plane[:, cols], y_bf16[:].rearrange("p j t -> p (j t)"))
+            y_bf16 = ring.tile([P, width, PACK], BF16, name="y_bf16", align_bytes=64)
+            round_and_interleave(nc, c not in Y_ON_VECTOR, y_bf16[:], y[:])
+            y_values[c] = y_bf16
+
+        def planes(c):
+            width = WIDTHS[c]
+            cols = slice(STARTS[c], STARTS[c] + width)
+            y_codes = ring.tile([P, width], I32, name="y_codes", align_bytes=64)
+            quantize(nc, y_codes[:], out_plane[:, cols], y_values[c][:])
             nc.sync.dma_start(out=out_words[:, cols], in_=y_codes[:])
 
+        def deal_w1():
+            deal(w1_codes, w1_raw_words)
+            deal(w1_plane, w1_raw_scales)
+
+        b_products(0)
+        deal_w1()
         for step in range(CHUNKS + 2):
-            if 0 <= step - 2 < CHUNKS:
-                hand_out(step - 2)
-            if 0 <= step - 1 < CHUNKS:
-                gated_product(step - 1)
             if step < CHUNKS:
-                first_products(step)
+                a_products(step)
+            if step + 1 < CHUNKS:
+                b_products(step + 1)
+            if 0 <= step - 2 < CHUNKS:
+                planes(step - 2)
+            if step < CHUNKS:
+                gated(step)
+            if 0 <= step - 1 < CHUNKS:
+                add_reg(step - 1)
+            if step < CHUNKS:
+                second_product(step)
 
         for q in range(4):
             queue = nc.sync if q % 2 == 0 else nc.scalar

@@ -21,7 +21,7 @@ LINE = 4
 WIDTHS = [128,128,128,128]
 STARTS = [sum(WIDTHS[:c]) for c in range(len(WIDTHS))]
 CHUNKS = len(WIDTHS)
-Y_ON_VECTOR = [0,3]
+Y_ON_VECTOR = [3]
 
 
 def round_and_interleave(nc, on_scalar, out, in_):
@@ -74,15 +74,15 @@ def tile_picked_regmix_relu_po_kernel(
         w1_raw_scales = keep.tile([P, N], U8, name="w1_raw_scales", align_bytes=64)
         gate = keep.tile([P, PACK], F32, name="gate")
 
-        wa_raw, wb_raw, reg_raw = {}, {}, {}
+        wa_raw = keep.tile([P, PACK, H], F32, name="wa_raw", align_bytes=64)
+        wb_raw = keep.tile([P, PACK, H], F32, name="wb_raw", align_bytes=64)
+        reg_raw = keep.tile([P, PACK, H], F32, name="reg_raw", align_bytes=64)
 
-        def load_chunks(rows, loaded, name, first, count):
-            lo = STARTS[first]
-            hi = STARTS[first + count - 1] + WIDTHS[first + count - 1]
-            raw = keep.tile([P, PACK, hi - lo], F32, name="%s%d" % (name, first), align_bytes=64)
-            nc.sync.dma_start(out=raw[:], in_=rows[:, :, lo:hi])
-            for c in range(first, first + count):
-                loaded[c] = raw[:, :, STARTS[c] - lo : STARTS[c] - lo + WIDTHS[c]]
+        def columns(c):
+            return slice(STARTS[c], STARTS[c] + WIDTHS[c])
+
+        def load_columns(raw, rows, lo, hi):
+            nc.sync.dma_start(out=raw[:, :, lo:hi], in_=rows[:, :, lo:hi])
 
         def load_scales(plane, scales):
             for q in range(4):
@@ -94,31 +94,31 @@ def tile_picked_regmix_relu_po_kernel(
         def load_words(table, words):
             nc.sync.dma_start(out=table[:], in_=words[0].rearrange("p c t -> p (c t)").bitcast(I32))
 
-        nc.vector.memset(x_scale_table[:, : T // 2].bitcast(I32), 0)
-        nc.gpsimd.memset(x_scale_table[:, T // 2 :].bitcast(I32), 0)
+        nc.vector.memset(x_scale_table[:].bitcast(I32), 0)
         nc.gpsimd.memset(w1_raw_scales[:].bitcast(I32), 0)
         nc.sync.dma_start(offsets[:], offs)
         nc.sync.dma_start(out=gate[:], in_=gt.rearrange("(p t) o -> p (t o)", t=PACK))
+        load_columns(wb_raw, wb_rows, 0, 128)
         load_scales(x_scale_table, x_scales)
-        load_chunks(wb_rows, wb_raw, "wb_raw", 0, 1)
         load_words(x_word_table, x_words)
-        load_chunks(wa_rows, wa_raw, "wa_raw", 0, 1)
-        load_chunks(wb_rows, wb_raw, "wb_raw", 1, 1)
-        load_chunks(wa_rows, wa_raw, "wa_raw", 1, 1)
+        load_columns(wa_raw, wa_rows, 0, 128)
+        load_columns(wb_raw, wb_rows, 128, 256)
+        load_columns(wa_raw, wa_rows, 128, 256)
         load_scales(w1_raw_scales, w1_scales)
         load_words(w1_raw_words, w1_words)
-        load_chunks(wb_rows, wb_raw, "wb_raw", 2, 1)
-        load_chunks(wa_rows, wa_raw, "wa_raw", 2, 1)
-        load_chunks(wb_rows, wb_raw, "wb_raw", 3, 1)
-        load_chunks(wa_rows, wa_raw, "wa_raw", 3, 1)
-        load_chunks(reg_rows, reg_raw, "reg_raw", 0, 2)
-        load_chunks(reg_rows, reg_raw, "reg_raw", 2, 2)
+        load_columns(wb_raw, wb_rows, 256, 384)
+        load_columns(wa_raw, wa_rows, 256, 384)
+        load_columns(wb_raw, wb_rows, 384, 512)
+        load_columns(wa_raw, wa_rows, 384, 512)
+        load_columns(reg_raw, reg_rows, 0, 256)
+        load_columns(reg_raw, reg_rows, 256, 512)
 
         picked_scales = keep.tile([P, S], U8, name="picked_scales", align_bytes=64)
         x_codes = keep.tile([P, S], U32, name="x_codes", align_bytes=64)
         x_plane = keep.tile([P, S], U8, name="x_plane", align_bytes=64)
         w1_codes = keep.tile([P, N], I32, name="w1_codes", align_bytes=64)
         w1_plane = keep.tile([P, N], U8, name="w1_plane", align_bytes=64)
+        out_codes = keep.tile([P, H], I32, name="out_codes", align_bytes=64)
         out_plane = keep.tile([P, H], U8, name="out_plane", align_bytes=64)
 
         def deal(out, in_):
@@ -134,13 +134,14 @@ def tile_picked_regmix_relu_po_kernel(
             in_=x_word_table[:].bitcast(U32).indirect(offsets[:]),
         )
 
-        a_banks, b_banks, z_values, products, y_values = {}, {}, {}, {}, {}
+        a_banks, b_banks, z_values, products, y_values, rounded = {}, {}, {}, {}, {}, {}
 
         def weight_products(raw, name, c):
             width = WIDTHS[c]
             w_bf16 = ring.tile([P, width, PACK], BF16, name=name + "_bf16", align_bytes=64)
             w_codes = ring.tile([P, width], U32, name=name + "_codes", align_bytes=64)
             w_plane = ring.tile([P, width], U8, name=name + "_plane", align_bytes=64)
+            rounded[name, c] = w_bf16
             round_and_interleave(nc, True, w_bf16[:], raw)
             quantize(nc, w_codes[:], w_plane[:], w_bf16[:])
             bank = psum_ab.tile([P, PACK, width], F32, name=name + "_bank")
@@ -148,14 +149,14 @@ def tile_picked_regmix_relu_po_kernel(
             return bank
 
         def b_products(c):
-            b_banks[c] = weight_products(wb_raw[c], "b", c)
+            b_banks[c] = weight_products(wb_raw[:, :, columns(c)], "b", c)
 
         def a_products(c):
-            a_banks[c] = weight_products(wa_raw[c], "a", c)
+            a_banks[c] = weight_products(wa_raw[:, :, columns(c)], "a", c)
 
         def gated(c):
             width = WIDTHS[c]
-            gated_b = wb_raw[(c + 1) % CHUNKS]
+            gated_b = wa_raw[:, :, columns((c + 1) % CHUNKS)]
             for t in range(PACK):
                 nc.scalar.activation(out=gated_b[:, t, :], in_=b_banks[c][:, t, :], func=COPY, scale=gate[:, t : t + 1])
             z_bf16 = ring.tile([P, width, PACK], BF16, name="z_bf16", align_bytes=64)
@@ -181,39 +182,40 @@ def tile_picked_regmix_relu_po_kernel(
         def add_reg(c):
             width = WIDTHS[c]
             cols = slice(STARTS[c], STARTS[c] + width)
-            y = ring.tile([P, PACK, width], F32, name="y", align_bytes=64)
-            nc.vector.tensor_tensor(out=y[:], in0=products[c][:], in1=reg_raw[c], op=ALU.add)
-            nc.sync.dma_start(out=out_rows[:, :, cols], in_=y[:])
-            y_bf16 = ring.tile([P, width, PACK], BF16, name="y_bf16", align_bytes=64)
-            round_and_interleave(nc, c not in Y_ON_VECTOR, y_bf16[:], y[:])
-            y_values[c] = y_bf16
+            y = wa_raw[:, :, columns((c + 2) % CHUNKS)]
+            nc.vector.tensor_tensor(out=y, in0=products[c][:], in1=reg_raw[:, :, columns(c)], op=ALU.add)
+            nc.sync.dma_start(out=out_rows[:, :, cols], in_=y)
+            y_values[c] = y
 
         def planes(c):
             width = WIDTHS[c]
             cols = slice(STARTS[c], STARTS[c] + width)
-            y_codes = ring.tile([P, width], I32, name="y_codes", align_bytes=64)
-            quantize(nc, y_codes[:], out_plane[:, cols], y_values[c][:])
-            nc.sync.dma_start(out=out_words[:, cols], in_=y_codes[:])
+            y_bf16 = rounded["a", (c - 1) % CHUNKS]
+            round_and_interleave(nc, c not in Y_ON_VECTOR, y_bf16[:], y_values[c])
+            quantize(nc, out_codes[:, cols], out_plane[:, cols], y_bf16[:])
+            if c % 2 == 1:
+                pair = slice(STARTS[c - 1], STARTS[c] + width)
+                nc.sync.dma_start(out=out_words[:, pair], in_=out_codes[:, pair])
 
         def deal_w1():
             deal(w1_codes, w1_raw_words)
             deal(w1_plane, w1_raw_scales)
 
         b_products(0)
-        deal_w1()
+        a_products(0)
         for step in range(CHUNKS + 2):
-            if step < CHUNKS:
-                a_products(step)
             if step + 1 < CHUNKS:
                 b_products(step + 1)
-            if 0 <= step - 2 < CHUNKS:
-                planes(step - 2)
+                a_products(step + 1)
             if step < CHUNKS:
                 gated(step)
+                if step == 0:
+                    deal_w1()
+                second_product(step)
             if 0 <= step - 1 < CHUNKS:
                 add_reg(step - 1)
-            if step < CHUNKS:
-                second_product(step)
+            if 0 <= step - 2 < CHUNKS:
+                planes(step - 2)
 
         for q in range(4):
             queue = nc.sync if q % 2 == 0 else nc.scalar

@@ -85,10 +85,10 @@ def tile_picked_regmix_relu_po_kernel(
             nc.sync.dma_start(out=raw[:, :, lo:hi], in_=rows[:, :, lo:hi])
 
         def load_scales(plane, scales):
-            for q in range(4):
+            for r in range(4):
                 nc.sync.dma_start(
-                    out=plane[32 * q : 32 * q + 4, :].bitcast(I32),
-                    in_=scales[0, 4 * q : 4 * q + 4, :].bitcast(I32),
+                    out=plane[r:P:32, :].bitcast(I32),
+                    in_=scales[0, r:16:4, :].bitcast(I32),
                 )
 
         def load_words(table, words):
@@ -114,12 +114,19 @@ def tile_picked_regmix_relu_po_kernel(
         load_columns(reg_raw, reg_rows, 256, 512)
 
         picked_scales = keep.tile([P, S], U8, name="picked_scales", align_bytes=64)
+        picked_words = keep.tile([P, S], U32, name="picked_words", align_bytes=64)
         x_codes = keep.tile([P, S], U32, name="x_codes", align_bytes=64)
         x_plane = keep.tile([P, S], U8, name="x_plane", align_bytes=64)
         w1_codes = keep.tile([P, N], I32, name="w1_codes", align_bytes=64)
         w1_plane = keep.tile([P, N], U8, name="w1_plane", align_bytes=64)
         out_codes = keep.tile([P, H], I32, name="out_codes", align_bytes=64)
         out_plane = keep.tile([P, H], U8, name="out_plane", align_bytes=64)
+
+        def deal_words(out, in_, slots):
+            nc.vector.tensor_copy(
+                out=out.rearrange("p (t c i) -> p c t i", t=PACK, i=LINE)[:, :, slots, :],
+                in_=in_.rearrange("p (c i t) -> p c t i", t=PACK, i=LINE)[:, :, slots, :],
+            )
 
         def deal(out, in_):
             nc.vector.tensor_copy(
@@ -129,10 +136,9 @@ def tile_picked_regmix_relu_po_kernel(
 
         nc.vector.tensor_copy(out=picked_scales[:], in_=x_scale_table[:].indirect(offsets[:]))
         deal(x_plane, picked_scales)
-        nc.vector.tensor_copy(
-            out=x_codes[:].rearrange("p (t m) -> p m t", t=PACK),
-            in_=x_word_table[:].bitcast(U32).indirect(offsets[:]),
-        )
+        nc.vector.tensor_copy(out=picked_words[:], in_=x_word_table[:].bitcast(U32).indirect(offsets[:]))
+        for half in range(2):
+            deal_words(x_codes[:].bitcast(I32), picked_words[:].bitcast(I32), slice(2 * half, 2 * half + 2))
 
         a_banks, b_banks, z_values, products, y_values, rounded = {}, {}, {}, {}, {}, {}
 
@@ -198,7 +204,7 @@ def tile_picked_regmix_relu_po_kernel(
                 nc.sync.dma_start(out=out_words[:, pair], in_=out_codes[:, pair])
 
         def deal_w1():
-            deal(w1_codes, w1_raw_words)
+            deal_words(w1_codes[:], w1_raw_words[:], slice(0, PACK))
             deal(w1_plane, w1_raw_scales)
 
         b_products(0)

@@ -17,35 +17,60 @@ ALU = mybir.AluOpType
 
 P = 128
 PACK = 4
-LINE = 4
-WIDTHS = [128,128,128,128]
-STARTS = [sum(WIDTHS[:c]) for c in range(len(WIDTHS))]
-CHUNKS = len(WIDTHS)
-Y_ON_VECTOR = [3]
+QUADRANT = 32
+SCALE_ROWS = 4
+RUN = 4
+CHUNK = 128
+CHUNKS = H // CHUNK
+HALF = 2 * CHUNK
+AB_BANKS = 3
+OUT_BANKS = 2
+
+
+def columns(c):
+    return slice(c * CHUNK, (c + 1) * CHUNK)
+
+
+def half_columns(h):
+    return slice(h * HALF, (h + 1) * HALF)
 
 
 def round_and_interleave(nc, on_scalar, out, in_):
-    dst = out.rearrange("p (c i) t -> p c t i", i=LINE)
-    src = in_.rearrange("p t (c i) -> p c t i", i=LINE)
+    dst = out.rearrange("p (c i) t -> p c t i", i=RUN)
+    src = in_.rearrange("p t (c i) -> p c t i", i=RUN)
     if on_scalar:
         nc.scalar.activation(out=dst, in_=src, func=COPY)
     else:
         nc.vector.tensor_copy(out=dst, in_=src)
 
 
-def quantize(nc, codes, scales, values):
-    nc.vector.quantize_mx(out=codes.bitcast(FP8X4), scales=scales, in_=values.rearrange("p j t -> p (j t)"))
+def quantize(nc, words, plane, values):
+    nc.vector.quantize_mx(out=words.bitcast(FP8X4), scales=plane, in_=values.rearrange("p j t -> p (j t)"))
 
 
-def four_products(nc, bank, lhs_codes, lhs_scales, rhs_codes, rhs_scales):
+def deal_words(nc, out, in_, slots):
+    nc.vector.tensor_copy(
+        out=out.rearrange("p (t c i) -> p c t i", t=PACK, i=RUN)[:, :, slots, :],
+        in_=in_.rearrange("p (c i t) -> p c t i", t=PACK, i=RUN)[:, :, slots, :],
+    )
+
+
+def deal_plane(nc, out, in_):
+    nc.vector.tensor_copy(
+        out=out.rearrange("p (t m) -> p t m", t=PACK),
+        in_=in_.rearrange("p (m t) -> p t m", t=PACK),
+    )
+
+
+def four_products(nc, bank, dealt_words, dealt_plane, moving_words, moving_plane):
     for t in range(PACK):
-        cols = slice(t * P, (t + 1) * P)
+        stationary = slice(t * P, (t + 1) * P)
         nc.tensor.matmul_mx(
             out=bank[:, t, :],
-            lhsT=lhs_codes[:, cols].bitcast(FP8X4),
-            lhsT_scale=lhs_scales[:, cols],
-            rhs=rhs_codes.bitcast(FP8X4),
-            rhs_scale=rhs_scales,
+            lhsT=dealt_words[:, stationary].bitcast(FP8X4),
+            lhsT_scale=dealt_plane[:, stationary],
+            rhs=moving_words.bitcast(FP8X4),
+            rhs_scale=moving_plane,
             start=True,
             stop=True,
         )
@@ -57,175 +82,147 @@ def tile_picked_regmix_relu_po_kernel(
     nc = tc.nc
     with ExitStack() as ctx:
         keep = ctx.enter_context(tc.tile_pool(name="keep", bufs=1))
-        ring = ctx.enter_context(tc.tile_pool(name="ring", bufs=CHUNKS))
-        psum_ab = ctx.enter_context(tc.psum_pool(name="psum_ab", bufs=3))
-        psum_o = ctx.enter_context(tc.psum_pool(name="psum_o", bufs=2))
+        per_chunk = ctx.enter_context(tc.tile_pool(name="per_chunk", bufs=CHUNKS))
+        per_half = ctx.enter_context(tc.tile_pool(name="per_half", bufs=H // HALF))
+        psum_ab = ctx.enter_context(tc.psum_pool(name="psum_ab", bufs=AB_BANKS))
+        psum_out = ctx.enter_context(tc.psum_pool(name="psum_out", bufs=OUT_BANKS))
 
         wa_rows = wa.rearrange("(p t) j -> p t j", t=PACK)
         wb_rows = wb.rearrange("(p t) j -> p t j", t=PACK)
         reg_rows = reg.rearrange("(p t) j -> p t j", t=PACK)
-        out_rows = out_0.rearrange("(p t) j -> p t j", t=PACK)
-        out_words = out_1[0].rearrange("p j t -> p (j t)").bitcast(I32)
+        out_0_rows = out_0.rearrange("(p t) j -> p t j", t=PACK)
+        out_1_words = out_1[0].rearrange("p j t -> p (j t)").bitcast(I32)
 
         offsets = keep.tile([P, S // 16], U16, name="offsets")
         x_word_table = keep.tile([P, T], I32, name="x_word_table", align_bytes=64)
         x_scale_table = keep.tile([P, T], U8, name="x_scale_table", align_bytes=64)
         w1_raw_words = keep.tile([P, N], I32, name="w1_raw_words", align_bytes=64)
-        w1_raw_scales = keep.tile([P, N], U8, name="w1_raw_scales", align_bytes=64)
+        w1_raw_plane = keep.tile([P, N], U8, name="w1_raw_plane", align_bytes=64)
         gate = keep.tile([P, PACK], F32, name="gate")
-
-        wa_raw = keep.tile([P, PACK, H], F32, name="wa_raw", align_bytes=64)
+        stage = keep.tile([P, PACK, H], F32, name="stage", align_bytes=64)
         wb_raw = keep.tile([P, PACK, H], F32, name="wb_raw", align_bytes=64)
         reg_raw = keep.tile([P, PACK, H], F32, name="reg_raw", align_bytes=64)
 
-        def columns(c):
-            return slice(STARTS[c], STARTS[c] + WIDTHS[c])
+        def load_half(raw, rows, h):
+            nc.sync.dma_start(out=raw[:, :, half_columns(h)], in_=rows[:, :, half_columns(h)])
 
-        def load_columns(raw, rows, lo, hi):
-            nc.sync.dma_start(out=raw[:, :, lo:hi], in_=rows[:, :, lo:hi])
-
-        def load_scales(plane, scales):
-            for r in range(4):
+        def load_plane(plane, scales):
+            for r in range(SCALE_ROWS):
                 nc.sync.dma_start(
-                    out=plane[r:P:32, :].bitcast(I32),
-                    in_=scales[0, r:16:4, :].bitcast(I32),
+                    out=plane[r:P:QUADRANT, :].bitcast(I32),
+                    in_=scales[0, r : K // QUADRANT : SCALE_ROWS, :].bitcast(I32),
                 )
 
         def load_words(table, words):
             nc.sync.dma_start(out=table[:], in_=words[0].rearrange("p c t -> p (c t)").bitcast(I32))
 
         nc.vector.memset(x_scale_table[:].bitcast(I32), 0)
-        nc.gpsimd.memset(w1_raw_scales[:].bitcast(I32), 0)
+        nc.gpsimd.memset(w1_raw_plane[:].bitcast(I32), 0)
+
         nc.sync.dma_start(offsets[:], offs)
         nc.sync.dma_start(out=gate[:], in_=gt.rearrange("(p t) o -> p (t o)", t=PACK))
-        load_columns(wb_raw, wb_rows, 0, 128)
-        load_scales(x_scale_table, x_scales)
+        load_half(wb_raw, wb_rows, 0)
+        load_plane(x_scale_table, x_scales)
         load_words(x_word_table, x_words)
-        load_columns(wa_raw, wa_rows, 0, 128)
-        load_columns(wb_raw, wb_rows, 128, 256)
-        load_columns(wa_raw, wa_rows, 128, 256)
-        load_scales(w1_raw_scales, w1_scales)
+        load_half(stage, wa_rows, 0)
+        load_plane(w1_raw_plane, w1_scales)
         load_words(w1_raw_words, w1_words)
-        load_columns(wb_raw, wb_rows, 256, 384)
-        load_columns(wa_raw, wa_rows, 256, 384)
-        load_columns(wb_raw, wb_rows, 384, 512)
-        load_columns(wa_raw, wa_rows, 384, 512)
-        load_columns(reg_raw, reg_rows, 0, 256)
-        load_columns(reg_raw, reg_rows, 256, 512)
+        load_half(wb_raw, wb_rows, 1)
+        load_half(stage, wa_rows, 1)
+        load_half(reg_raw, reg_rows, 0)
+        load_half(reg_raw, reg_rows, 1)
 
-        picked_scales = keep.tile([P, S], U8, name="picked_scales", align_bytes=64)
+        picked_plane = keep.tile([P, S], U8, name="picked_plane", align_bytes=64)
         picked_words = keep.tile([P, S], U32, name="picked_words", align_bytes=64)
-        x_codes = keep.tile([P, S], U32, name="x_codes", align_bytes=64)
-        x_plane = keep.tile([P, S], U8, name="x_plane", align_bytes=64)
-        w1_codes = keep.tile([P, N], I32, name="w1_codes", align_bytes=64)
-        w1_plane = keep.tile([P, N], U8, name="w1_plane", align_bytes=64)
-        out_codes = keep.tile([P, H], I32, name="out_codes", align_bytes=64)
-        out_plane = keep.tile([P, H], U8, name="out_plane", align_bytes=64)
+        x_dealt_words = keep.tile([P, S], U32, name="x_dealt_words", align_bytes=64)
+        x_dealt_plane = keep.tile([P, S], U8, name="x_dealt_plane", align_bytes=64)
+        w1_dealt_words = keep.tile([P, N], I32, name="w1_dealt_words", align_bytes=64)
+        w1_dealt_plane = keep.tile([P, N], U8, name="w1_dealt_plane", align_bytes=64)
+        result_words = keep.tile([P, H], I32, name="result_words", align_bytes=64)
+        result_plane = keep.tile([P, H], U8, name="result_plane", align_bytes=64)
 
-        def deal_words(out, in_, slots):
-            nc.vector.tensor_copy(
-                out=out.rearrange("p (t c i) -> p c t i", t=PACK, i=LINE)[:, :, slots, :],
-                in_=in_.rearrange("p (c i t) -> p c t i", t=PACK, i=LINE)[:, :, slots, :],
-            )
-
-        def deal(out, in_):
-            nc.vector.tensor_copy(
-                out=out[:].rearrange("p (t m) -> p t m", t=PACK),
-                in_=in_[:].rearrange("p (m t) -> p t m", t=PACK),
-            )
-
-        nc.vector.tensor_copy(out=picked_scales[:], in_=x_scale_table[:].indirect(offsets[:]))
-        deal(x_plane, picked_scales)
+        nc.vector.tensor_copy(out=picked_plane[:], in_=x_scale_table[:].indirect(offsets[:]))
+        deal_plane(nc, x_dealt_plane[:], picked_plane[:])
         nc.vector.tensor_copy(out=picked_words[:], in_=x_word_table[:].bitcast(U32).indirect(offsets[:]))
-        for half in range(2):
-            deal_words(x_codes[:].bitcast(I32), picked_words[:].bitcast(I32), slice(2 * half, 2 * half + 2))
+        for first in range(0, PACK, 2):
+            deal_words(nc, x_dealt_words[:].bitcast(I32), picked_words[:].bitcast(I32), slice(first, first + 2))
 
-        a_banks, b_banks, z_values, products, y_values, rounded = {}, {}, {}, {}, {}, {}
+        banks, rounded, out_banks = {}, {}, {}
 
-        def weight_products(raw, name, c):
-            width = WIDTHS[c]
-            w_bf16 = ring.tile([P, width, PACK], BF16, name=name + "_bf16", align_bytes=64)
-            w_codes = ring.tile([P, width], U32, name=name + "_codes", align_bytes=64)
-            w_plane = ring.tile([P, width], U8, name=name + "_plane", align_bytes=64)
-            rounded[name, c] = w_bf16
-            round_and_interleave(nc, True, w_bf16[:], raw)
-            quantize(nc, w_codes[:], w_plane[:], w_bf16[:])
-            bank = psum_ab.tile([P, PACK, width], F32, name=name + "_bank")
-            four_products(nc, bank, x_codes, x_plane, w_codes[:], w_plane[:])
-            return bank
+        def token_products(raw, name, h):
+            w_bf16 = per_half.tile([P, HALF, PACK], BF16, name=name + "_bf16", align_bytes=64)
+            w_words = per_half.tile([P, HALF], U32, name=name + "_words", align_bytes=64)
+            w_plane = per_half.tile([P, HALF], U8, name=name + "_plane", align_bytes=64)
+            rounded[name, h] = w_bf16
+            round_and_interleave(nc, True, w_bf16[:], raw[:, :, half_columns(h)])
+            quantize(nc, w_words[:], w_plane[:], w_bf16[:])
+            for s in range(HALF // CHUNK):
+                bank = psum_ab.tile([P, PACK, CHUNK], F32, name=name + "_bank")
+                four_products(nc, bank, x_dealt_words, x_dealt_plane, w_words[:, columns(s)], w_plane[:, columns(s)])
+                banks[name, 2 * h + s] = bank
 
-        def b_products(c):
-            b_banks[c] = weight_products(wb_raw[:, :, columns(c)], "b", c)
-
-        def a_products(c):
-            a_banks[c] = weight_products(wa_raw[:, :, columns(c)], "a", c)
-
-        def gated(c):
-            width = WIDTHS[c]
-            gated_b = wa_raw[:, :, columns((c + 1) % CHUNKS)]
+        def gate_chunk(c):
+            gated_b = stage[:, :, columns(c ^ 1)]
             for t in range(PACK):
-                nc.scalar.activation(out=gated_b[:, t, :], in_=b_banks[c][:, t, :], func=COPY, scale=gate[:, t : t + 1])
-            z_bf16 = ring.tile([P, width, PACK], BF16, name="z_bf16", align_bytes=64)
+                nc.scalar.activation(out=gated_b[:, t, :], in_=banks["b", c][:, t, :], func=COPY, scale=gate[:, t : t + 1])
+            z_bf16 = per_chunk.tile([P, CHUNK, PACK], BF16, name="z_bf16", align_bytes=64)
             nc.vector.scalar_tensor_tensor(
                 out=z_bf16[:],
-                in0=a_banks[c][:].rearrange("p t j -> p j t"),
+                in0=banks["a", c][:].rearrange("p t j -> p j t"),
                 scalar=0.0,
                 in1=gated_b.rearrange("p t j -> p j t"),
                 op0=ALU.max,
                 op1=ALU.mult,
             )
-            z_values[c] = z_bf16
+            return z_bf16
 
-        def second_product(c):
-            width = WIDTHS[c]
-            z_codes = ring.tile([P, width], U32, name="z_codes", align_bytes=64)
-            z_plane = ring.tile([P, width], U8, name="z_plane", align_bytes=64)
-            quantize(nc, z_codes[:], z_plane[:], z_values[c][:])
-            o_bank = psum_o.tile([P, PACK, width], F32, name="o_bank")
-            four_products(nc, o_bank, w1_codes, w1_plane, z_codes[:], z_plane[:])
-            products[c] = o_bank
+        def register_products(c, z_bf16):
+            z_words = per_chunk.tile([P, CHUNK], U32, name="z_words", align_bytes=64)
+            z_plane = per_chunk.tile([P, CHUNK], U8, name="z_plane", align_bytes=64)
+            quantize(nc, z_words[:], z_plane[:], z_bf16[:])
+            out_bank = psum_out.tile([P, PACK, CHUNK], F32, name="out_bank")
+            four_products(nc, out_bank, w1_dealt_words, w1_dealt_plane, z_words[:], z_plane[:])
+            out_banks[c] = out_bank
 
         def add_reg(c):
-            width = WIDTHS[c]
-            cols = slice(STARTS[c], STARTS[c] + width)
-            y = wa_raw[:, :, columns((c + 2) % CHUNKS)]
-            nc.vector.tensor_tensor(out=y, in0=products[c][:], in1=reg_raw[:, :, columns(c)], op=ALU.add)
-            nc.sync.dma_start(out=out_rows[:, :, cols], in_=y)
-            y_values[c] = y
+            nc.vector.tensor_tensor(
+                out=stage[:, :, columns(c)], in0=out_banks[c][:], in1=reg_raw[:, :, columns(c)], op=ALU.add
+            )
 
-        def planes(c):
-            width = WIDTHS[c]
-            cols = slice(STARTS[c], STARTS[c] + width)
-            y_bf16 = rounded["a", (c - 1) % CHUNKS]
-            round_and_interleave(nc, c not in Y_ON_VECTOR, y_bf16[:], y_values[c])
-            quantize(nc, out_codes[:, cols], out_plane[:, cols], y_bf16[:])
+        def store_out_0(cols):
+            nc.sync.dma_start(out=out_0_rows[:, :, cols], in_=stage[:, :, cols])
+
+        def quantize_result(c):
+            y_bf16 = rounded["a", 1 - c // 2][:, columns(c % 2), :]
+            round_and_interleave(nc, c < CHUNKS - 1, y_bf16, stage[:, :, columns(c)])
+            quantize(nc, result_words[:, columns(c)], result_plane[:, columns(c)], y_bf16)
             if c % 2 == 1:
-                pair = slice(STARTS[c - 1], STARTS[c] + width)
-                nc.sync.dma_start(out=out_words[:, pair], in_=out_codes[:, pair])
+                cols = half_columns(c // 2)
+                nc.sync.dma_start(out=out_1_words[:, cols], in_=result_words[:, cols])
 
-        def deal_w1():
-            deal_words(w1_codes[:], w1_raw_words[:], slice(0, PACK))
-            deal(w1_plane, w1_raw_scales)
+        token_products(wb_raw, "b", 0)
+        token_products(stage, "a", 0)
+        first_z = gate_chunk(0)
+        deal_words(nc, w1_dealt_words[:], w1_raw_words[:], slice(0, PACK))
+        deal_plane(nc, w1_dealt_plane[:], w1_raw_plane[:])
+        register_products(0, first_z)
+        register_products(1, gate_chunk(1))
+        token_products(wb_raw, "b", 1)
+        token_products(stage, "a", 1)
+        add_reg(0)
+        add_reg(1)
+        store_out_0(half_columns(0))
+        register_products(2, gate_chunk(2))
+        register_products(3, gate_chunk(3))
+        for c in (2, 3):
+            add_reg(c)
+            store_out_0(columns(c))
+        for c in range(CHUNKS):
+            quantize_result(c)
 
-        b_products(0)
-        a_products(0)
-        for step in range(CHUNKS + 2):
-            if step + 1 < CHUNKS:
-                b_products(step + 1)
-                a_products(step + 1)
-            if step < CHUNKS:
-                gated(step)
-                if step == 0:
-                    deal_w1()
-                second_product(step)
-            if 0 <= step - 1 < CHUNKS:
-                add_reg(step - 1)
-            if 0 <= step - 2 < CHUNKS:
-                planes(step - 2)
-
-        for q in range(4):
+        for q in range(P // QUADRANT):
             queue = nc.sync if q % 2 == 0 else nc.scalar
             queue.dma_start(
-                out=out_2[0, 4 * q : 4 * q + 4, :].bitcast(I32),
-                in_=out_plane[32 * q : 32 * q + 4, :].bitcast(I32),
+                out=out_2[0, SCALE_ROWS * q : SCALE_ROWS * (q + 1), :].bitcast(I32),
+                in_=result_plane[QUADRANT * q : QUADRANT * q + SCALE_ROWS, :].bitcast(I32),
             )

from contextlib import ExitStack

import concourse.mybir as mybir

K, T, S, N, H = 512, 2048, 512, 512, 512
FLOPS = 2 * S * K * H * 2 + 2 * S * N * H

F32 = mybir.dt.float32
BF16 = mybir.dt.bfloat16
I32 = mybir.dt.int32
U32 = mybir.dt.uint32
U16 = mybir.dt.uint16
U8 = mybir.dt.uint8
FP8X4 = mybir.dt.float8_e4m3fn_x4
COPY = mybir.ActivationFunctionType.Copy
ALU = mybir.AluOpType

P = 128
PACK = 4
QUADRANT = 32
SCALE_ROWS = 4
RUN = 4
CHUNK = 128
CHUNKS = H // CHUNK
HALF = 2 * CHUNK
AB_BANKS = 3
OUT_BANKS = 2


def columns(c):
    return slice(c * CHUNK, (c + 1) * CHUNK)


def half_columns(h):
    return slice(h * HALF, (h + 1) * HALF)


def round_and_interleave(nc, on_scalar, out, in_):
    dst = out.rearrange("p (c i) t -> p c t i", i=RUN)
    src = in_.rearrange("p t (c i) -> p c t i", i=RUN)
    if on_scalar:
        nc.scalar.activation(out=dst, in_=src, func=COPY)
    else:
        nc.vector.tensor_copy(out=dst, in_=src)


def quantize(nc, words, plane, values):
    nc.vector.quantize_mx(out=words.bitcast(FP8X4), scales=plane, in_=values.rearrange("p j t -> p (j t)"))


def deal_words(nc, out, in_, slots):
    nc.vector.tensor_copy(
        out=out.rearrange("p (t c i) -> p c t i", t=PACK, i=RUN)[:, :, slots, :],
        in_=in_.rearrange("p (c i t) -> p c t i", t=PACK, i=RUN)[:, :, slots, :],
    )


def deal_plane(nc, out, in_):
    nc.vector.tensor_copy(
        out=out.rearrange("p (t m) -> p t m", t=PACK),
        in_=in_.rearrange("p (m t) -> p t m", t=PACK),
    )


def four_products(nc, bank, dealt_words, dealt_plane, moving_words, moving_plane):
    for t in range(PACK):
        stationary = slice(t * P, (t + 1) * P)
        nc.tensor.matmul_mx(
            out=bank[:, t, :],
            lhsT=dealt_words[:, stationary].bitcast(FP8X4),
            lhsT_scale=dealt_plane[:, stationary],
            rhs=moving_words.bitcast(FP8X4),
            rhs_scale=moving_plane,
            start=True,
            stop=True,
        )


def tile_picked_regmix_relu_po_kernel(
    tc, x_words, x_scales, wa, wb, gt, reg, w1_words, w1_scales, offs, out_0, out_1, out_2
):
    nc = tc.nc
    with ExitStack() as ctx:
        keep = ctx.enter_context(tc.tile_pool(name="keep", bufs=1))
        per_chunk = ctx.enter_context(tc.tile_pool(name="per_chunk", bufs=CHUNKS))
        per_half = ctx.enter_context(tc.tile_pool(name="per_half", bufs=H // HALF))
        psum_ab = ctx.enter_context(tc.psum_pool(name="psum_ab", bufs=AB_BANKS))
        psum_out = ctx.enter_context(tc.psum_pool(name="psum_out", bufs=OUT_BANKS))

        wa_rows = wa.rearrange("(p t) j -> p t j", t=PACK)
        wb_rows = wb.rearrange("(p t) j -> p t j", t=PACK)
        reg_rows = reg.rearrange("(p t) j -> p t j", t=PACK)
        out_0_rows = out_0.rearrange("(p t) j -> p t j", t=PACK)
        out_1_words = out_1[0].rearrange("p j t -> p (j t)").bitcast(I32)

        offsets = keep.tile([P, S // 16], U16, name="offsets")
        x_word_table = keep.tile([P, T], I32, name="x_word_table", align_bytes=64)
        x_scale_table = keep.tile([P, T], U8, name="x_scale_table", align_bytes=64)
        w1_raw_words = keep.tile([P, N], I32, name="w1_raw_words", align_bytes=64)
        w1_raw_plane = keep.tile([P, N], U8, name="w1_raw_plane", align_bytes=64)
        gate = keep.tile([P, PACK], F32, name="gate")
        stage = keep.tile([P, PACK, H], F32, name="stage", align_bytes=64)
        wb_raw = keep.tile([P, PACK, H], F32, name="wb_raw", align_bytes=64)
        reg_raw = keep.tile([P, PACK, H], F32, name="reg_raw", align_bytes=64)

        def load_half(raw, rows, h):
            nc.sync.dma_start(out=raw[:, :, half_columns(h)], in_=rows[:, :, half_columns(h)])

        def load_plane(plane, scales):
            for r in range(SCALE_ROWS):
                nc.sync.dma_start(
                    out=plane[r:P:QUADRANT, :].bitcast(I32),
                    in_=scales[0, r : K // QUADRANT : SCALE_ROWS, :].bitcast(I32),
                )

        def load_words(table, words):
            nc.sync.dma_start(out=table[:], in_=words[0].rearrange("p c t -> p (c t)").bitcast(I32))

        nc.vector.memset(x_scale_table[:].bitcast(I32), 0)
        nc.gpsimd.memset(w1_raw_plane[:].bitcast(I32), 0)

        nc.sync.dma_start(offsets[:], offs)
        nc.sync.dma_start(out=gate[:], in_=gt.rearrange("(p t) o -> p (t o)", t=PACK))
        load_half(wb_raw, wb_rows, 0)
        load_plane(x_scale_table, x_scales)
        load_words(x_word_table, x_words)
        load_half(stage, wa_rows, 0)
        load_plane(w1_raw_plane, w1_scales)
        load_words(w1_raw_words, w1_words)
        load_half(wb_raw, wb_rows, 1)
        load_half(stage, wa_rows, 1)
        load_half(reg_raw, reg_rows, 0)
        load_half(reg_raw, reg_rows, 1)

        picked_plane = keep.tile([P, S], U8, name="picked_plane", align_bytes=64)
        picked_words = keep.tile([P, S], U32, name="picked_words", align_bytes=64)
        x_dealt_words = keep.tile([P, S], U32, name="x_dealt_words", align_bytes=64)
        x_dealt_plane = keep.tile([P, S], U8, name="x_dealt_plane", align_bytes=64)
        w1_dealt_words = keep.tile([P, N], I32, name="w1_dealt_words", align_bytes=64)
        w1_dealt_plane = keep.tile([P, N], U8, name="w1_dealt_plane", align_bytes=64)
        result_words = keep.tile([P, H], I32, name="result_words", align_bytes=64)
        result_plane = keep.tile([P, H], U8, name="result_plane", align_bytes=64)

        nc.vector.tensor_copy(out=picked_plane[:], in_=x_scale_table[:].indirect(offsets[:]))
        deal_plane(nc, x_dealt_plane[:], picked_plane[:])
        nc.vector.tensor_copy(out=picked_words[:], in_=x_word_table[:].bitcast(U32).indirect(offsets[:]))
        for first in range(0, PACK, 2):
            deal_words(nc, x_dealt_words[:].bitcast(I32), picked_words[:].bitcast(I32), slice(first, first + 2))

        banks, rounded, out_banks = {}, {}, {}

        def token_products(raw, name, h):
            w_bf16 = per_half.tile([P, HALF, PACK], BF16, name=name + "_bf16", align_bytes=64)
            w_words = per_half.tile([P, HALF], U32, name=name + "_words", align_bytes=64)
            w_plane = per_half.tile([P, HALF], U8, name=name + "_plane", align_bytes=64)
            rounded[name, h] = w_bf16
            round_and_interleave(nc, True, w_bf16[:], raw[:, :, half_columns(h)])
            quantize(nc, w_words[:], w_plane[:], w_bf16[:])
            for s in range(HALF // CHUNK):
                bank = psum_ab.tile([P, PACK, CHUNK], F32, name=name + "_bank")
                four_products(nc, bank, x_dealt_words, x_dealt_plane, w_words[:, columns(s)], w_plane[:, columns(s)])
                banks[name, 2 * h + s] = bank

        def gate_chunk(c):
            gated_b = stage[:, :, columns(c ^ 1)]
            for t in range(PACK):
                nc.scalar.activation(out=gated_b[:, t, :], in_=banks["b", c][:, t, :], func=COPY, scale=gate[:, t : t + 1])
            z_bf16 = per_chunk.tile([P, CHUNK, PACK], BF16, name="z_bf16", align_bytes=64)
            nc.vector.scalar_tensor_tensor(
                out=z_bf16[:],
                in0=banks["a", c][:].rearrange("p t j -> p j t"),
                scalar=0.0,
                in1=gated_b.rearrange("p t j -> p j t"),
                op0=ALU.max,
                op1=ALU.mult,
            )
            return z_bf16

        def register_products(c, z_bf16):
            z_words = per_chunk.tile([P, CHUNK], U32, name="z_words", align_bytes=64)
            z_plane = per_chunk.tile([P, CHUNK], U8, name="z_plane", align_bytes=64)
            quantize(nc, z_words[:], z_plane[:], z_bf16[:])
            out_bank = psum_out.tile([P, PACK, CHUNK], F32, name="out_bank")
            four_products(nc, out_bank, w1_dealt_words, w1_dealt_plane, z_words[:], z_plane[:])
            out_banks[c] = out_bank

        def add_reg(c):
            nc.vector.tensor_tensor(
                out=stage[:, :, columns(c)], in0=out_banks[c][:], in1=reg_raw[:, :, columns(c)], op=ALU.add
            )

        def store_out_0(cols):
            nc.sync.dma_start(out=out_0_rows[:, :, cols], in_=stage[:, :, cols])

        def quantize_result(c):
            y_bf16 = rounded["a", 1 - c // 2][:, columns(c % 2), :]
            round_and_interleave(nc, c < CHUNKS - 1, y_bf16, stage[:, :, columns(c)])
            quantize(nc, result_words[:, columns(c)], result_plane[:, columns(c)], y_bf16)
            if c % 2 == 1:
                cols = half_columns(c // 2)
                nc.sync.dma_start(out=out_1_words[:, cols], in_=result_words[:, cols])

        token_products(wb_raw, "b", 0)
        token_products(stage, "a", 0)
        first_z = gate_chunk(0)
        deal_words(nc, w1_dealt_words[:], w1_raw_words[:], slice(0, PACK))
        deal_plane(nc, w1_dealt_plane[:], w1_raw_plane[:])
        register_products(0, first_z)
        register_products(1, gate_chunk(1))
        token_products(wb_raw, "b", 1)
        token_products(stage, "a", 1)
        add_reg(0)
        add_reg(1)
        store_out_0(half_columns(0))
        register_products(2, gate_chunk(2))
        register_products(3, gate_chunk(3))
        for c in (2, 3):
            add_reg(c)
            store_out_0(columns(c))
        for c in range(CHUNKS):
            quantize_result(c)

        for q in range(P // QUADRANT):
            queue = nc.sync if q % 2 == 0 else nc.scalar
            queue.dma_start(
                out=out_2[0, SCALE_ROWS * q : SCALE_ROWS * (q + 1), :].bitcast(I32),
                in_=result_plane[QUADRANT * q : QUADRANT * q + SCALE_ROWS, :].bitcast(I32),
            )
